import numpy as np
import ml_dtypes


def mxq(x, axis, fmt="e4m3"):
    dtype, down = {"e4m3": (ml_dtypes.float8_e4m3fn, 7), "e5m2": (ml_dtypes.float8_e5m2, 14)}[fmt]
    v = np.moveaxis(np.asarray(x, np.float32).astype(ml_dtypes.bfloat16).astype(np.float64), axis, -1)
    blocks = v.reshape(v.shape[:-1] + (-1, 32))
    amax = np.abs(blocks).max(-1, keepdims=True)
    byte = np.maximum(np.where(amax > 0, np.frexp(amax)[1] - 1 + 127, 0) - down, 1)
    scale = np.exp2(byte - 127.0)
    codes = (blocks / scale).astype(np.float32).astype(dtype).astype(np.float64)
    return np.moveaxis((codes * scale).reshape(v.shape), -1, axis)


WIDE = False


def mx_kscale(k):
    if not WIDE:
        return np.ones(k)
    levels = np.array([10, -10, 5, -5, 0])
    if k % 512:
        return np.exp2(np.random.permutation(np.resize(levels, k // 32))).repeat(32)
    a = np.empty((k // 512, 16))
    for p in range(k // 512):
        a[p, :8] = np.random.permutation(np.resize(levels, 8))
        for g in range(8):
            far = levels[np.abs(levels - a[p, g]) >= 10]
            a[p, g + 8] = far[np.random.randint(len(far))]
    return np.exp2(a.ravel()).repeat(32)


def f64(x):
    return np.asarray(x).astype(np.float64)


def striped(idx):
    return np.tile(idx.reshape(-1, 16).T, (8, 1)).astype(np.uint16)


def unstriped(offs):
    return offs[:16].T.reshape(-1).astype(np.int64)


def striped8(idx):
    return np.concatenate([x.reshape(-1, 16).T for x in idx]).astype(np.uint16)


def runs(offs, k):
    lists = np.stack([offs[16 * r : 16 * r + 16].T.reshape(-1) for r in range(8)]).astype(np.int64)
    return lists[np.arange(k) % 512 // 64]


def pack_weight(w):
    k, n = w.shape
    w = f64(np.asarray(w, np.float32).astype(ml_dtypes.bfloat16)).reshape(k // 32, 32, n)
    amax = np.abs(w).max(1)
    byte = np.clip(np.where(amax > 0, np.frexp(amax)[1] - 1 + 127 - 7, 1), 1, 254)
    scaled = (w * np.exp2(127.0 - byte)[:, None, :]).reshape(k, n).astype(np.float32)
    words = np.ascontiguousarray(scaled.reshape(k // 512, 128, 4, n).transpose(0, 1, 3, 2)).astype(ml_dtypes.float8_e4m3fn).view(np.uint8)
    return words, np.ascontiguousarray(byte.astype(np.uint8).reshape(k // 512, 16, n))


def unpack_weight(words, scales):
    g, p, n, _ = words.shape
    vals = np.ascontiguousarray(words).view(ml_dtypes.float8_e4m3fn).astype(np.float64) * np.repeat(np.exp2(scales.astype(np.float64) - 127.0), 8, axis=1)[..., None]
    return vals.transpose(0, 1, 3, 2).reshape(g * 512, n)


def relu(v):
    return np.maximum(v, 0.0)

def planes(y):
    n, m = y.shape
    v = y.astype(np.float32).astype(ml_dtypes.bfloat16).astype(np.float64).reshape(n // 32, 32, m)
    top = np.abs(v).max(1)
    byte = np.clip(np.where(top > 0, np.frexp(top)[1] - 1 + 127 - 7, 1), 1, 254)
    codes = (v * np.exp2(127.0 - byte)[:, None, :]).reshape(n, m).astype(np.float32).astype(ml_dtypes.float8_e4m3fn).view(np.uint8)
    words = codes.reshape(n // 512, 128, 4, m).transpose(0, 1, 3, 2)
    return np.ascontiguousarray(words), np.ascontiguousarray(byte.astype(np.uint8).reshape(n // 512, 16, m))


K, T, S, N, H, W = 512, 2048, 512, 512, 512, 256


def setup_inputs():
    n = np.random.standard_normal
    s = mx_kscale(K)[:, None]
    u = mx_kscale(H)
    packed_xT = pack_weight(n((K, T)) * s)
    packed_w1 = pack_weight(n((K, H)) / np.sqrt(K) / s)
    packed_w2 = pack_weight(n((H, N)) / np.sqrt(2 * H) / u[:, None])
    packed_w3 = pack_weight(n((K, N)) / np.sqrt(2 * K) / s)
    perm = np.stack([np.random.permutation(S) for _ in range(8)])
    return {
        "x_words": packed_xT[0],
        "x_scales": packed_xT[1],
        "w1_words": packed_w1[0],
        "w1_scales": packed_w1[1],
        "gn": (np.random.uniform(0.5, 1.5, (H, 1)) * u[:, None]).astype(np.float32),
        "w2_words": packed_w2[0],
        "w2_scales": packed_w2[1],
        "w3_words": packed_w3[0],
        "w3_scales": packed_w3[1],
        "offs": striped(np.random.permutation(T)[:S]),
        "n1": striped8(perm[:, :W]),
        "n2": striped8(perm[:, W:]),
        "two": striped(np.random.permutation(T)[:S]),
        "n3": striped8(np.stack([np.random.permutation(S) for _ in range(8)])),
        "n4": striped8(np.stack([np.random.permutation(S) for _ in range(8)])),
    }


def reference(x_words, x_scales, w1_words, w1_scales, gn, w2_words, w2_scales, w3_words, w3_scales, offs, n1, n2, two, n3, n4):
    xq = unpack_weight(x_words, x_scales)[:, unstriped(offs)]
    y = unpack_weight(w1_words, w1_scales).T @ xq
    pa = y[np.arange(H)[:, None], runs(n1, H)]
    pb = y[np.arange(H)[:, None], runs(n2, H)]
    rb = np.minimum(pa, pb)
    ra = np.maximum(pa, pb)
    ds = np.zeros((H, S))
    ds[np.arange(H)[:, None], runs(n1, H)] = ra
    dt = ds.copy()
    dt[np.arange(H)[:, None], runs(n2, H)] = rb
    z = f64(gn) * dt
    x_two = unpack_weight(x_words, x_scales)[:, unstriped(two)]
    h = unpack_weight(w2_words, w2_scales).T @ mxq(z, 0, "e4m3") + unpack_weight(w3_words, w3_scales).T @ x_two
    pa2 = h - (h[np.arange(N)[:, None], runs(n3, N)])
    pb2 = h[np.arange(N)[:, None], runs(n4, N)] - h
    out_0 = relu(np.minimum(pa2, pb2)) - (relu(-1.0 * np.maximum(pa2, pb2)))
    return (out_0,) + planes(out_0)

@@ -1,0 +1,213 @@
+from contextlib import ExitStack
+
+import concourse.mybir as mybir
+
+F32 = mybir.dt.float32
+BF16 = mybir.dt.bfloat16
+I32 = mybir.dt.int32
+U32 = mybir.dt.uint32
+U16 = mybir.dt.uint16
+U8 = mybir.dt.uint8
+FP8X4 = mybir.dt.float8_e4m3fn_x4
+ALU = mybir.AluOpType
+COPY = mybir.ActivationFunctionType.Copy
+
+P = 128
+PACK = 4
+T = 2048
+S = 512
+W = 256
+FLOPS = 3 * 2 * 512 * 512 * 512
+
+SLOT_ORDER = (2, 0, 1, 3)
+CHUNKS = ((0, 256), (256, 512))
+HALF = 256
+ON_VECTOR = ((0, 1, 0), (0, 1, 1))
+
+
+def tile_picked_mixinorderminmod_none_po_kernel(tc, x_words, x_scales, w1_words, w1_scales, gn, w2_words, w2_scales, w3_words, w3_scales,
+                        offs, n1, n2, two, n3, n4, out_0, out_1, out_2):
+    nc = tc.nc
+
+    def words_view(dram):
+        return dram[0].rearrange("p n t -> p (n t)").bitcast(I32)
+
+    def load_scale_rows(queue, tile, first_row, dram):
+        for q in range(4):
+            queue.dma_start(out=tile[32 * q + first_row : 32 * q + first_row + 4, :].bitcast(I32),
+                            in_=dram[0][4 * q : 4 * q + 4, :].bitcast(I32))
+
+    def deal(dst, src, lo, hi):
+        nc.vector.tensor_copy(out=dst[:].rearrange("p (t m) -> p t m", t=PACK)[:, lo:hi, :],
+                              in_=src[:].rearrange("p (m t) -> p t m", t=PACK)[:, lo:hi, :])
+
+    with ExitStack() as ctx:
+        lists = ctx.enter_context(tc.tile_pool(name="lists", bufs=1))
+        keep = ctx.enter_context(tc.tile_pool(name="keep", bufs=1))
+        ring = ctx.enter_context(tc.tile_pool(name="ring", bufs=2))
+        psum = ctx.enter_context(tc.psum_pool(name="psum", bufs=1))
+
+        def list_tile(dram, name):
+            tile = lists.tile([P, dram.shape[1]], U16, name=name)
+            nc.sync.dma_start(tile[:], dram)
+            return tile
+
+        xs = keep.tile([P, T], U8, name="xs", align_bytes=64)
+        w1s_raw = keep.tile([P, S], U8, name="w1s_raw", align_bytes=64)
+        w23s_raw = keep.tile([P, S], U8, name="w23s_raw", align_bytes=64)
+        nc.vector.memset(xs[:, 0 : T // 2].bitcast(I32), 0)
+        nc.gpsimd.memset(xs[:, T // 2 : T].bitcast(I32), 0)
+        nc.gpsimd.memset(w23s_raw[:].bitcast(I32), 0)
+
+        def load_w1_scales(queue, q):
+            rows = w1_scales[0][4 * q : 4 * q + 4, :].bitcast(I32)
+            queue.dma_start(out=w1s_raw[32 * q : 32 * q + 32, :].bitcast(I32), in_=rows.unsqueeze(0).to_broadcast([8, 4, S // 4]))
+
+        offs_t = list_tile(offs, "offs_t")
+        load_w1_scales(nc.scalar, 0)
+        load_w1_scales(nc.scalar, 1)
+        xw = keep.tile([P, T], I32, name="xw", align_bytes=64)
+        nc.scalar.dma_start(out=xw[:], in_=words_view(x_words))
+        load_scale_rows(nc.sync, xs, 0, x_scales)
+        load_w1_scales(nc.sync, 2)
+        load_w1_scales(nc.sync, 3)
+        w_raw = [keep.tile([P, S], I32, name="w_raw%d" % i, align_bytes=64) for i in range(3)]
+        for i, words in ((0, w1_words), (2, w3_words), (1, w2_words)):
+            nc.scalar.dma_start(out=w_raw[i][:], in_=words_view(words))
+        two_t = list_tile(two, "two_t")
+        n1_t = list_tile(n1, "n1_t")
+        n2_t = list_tile(n2, "n2_t")
+        load_scale_rows(nc.sync, w23s_raw, 0, w2_scales)
+        load_scale_rows(nc.sync, w23s_raw, 4, w3_scales)
+        gain = keep.tile([P, PACK], F32, name="gain")
+        nc.sync.dma_start(out=gain[:], in_=gn.rearrange("(p t) o -> p (t o)", t=PACK))
+        n3_t = list_tile(n3, "n3_t")
+        n4_t = list_tile(n4, "n4_t")
+
+        xa_s = keep.tile([P, S], U8, name="xa_s", align_bytes=64)
+        xb_s = keep.tile([P, S], U8, name="xb_s", align_bytes=64)
+        xa_w = keep.tile([P, S], U32, name="xa_w", align_bytes=64)
+        xb_w = keep.tile([P, S], U32, name="xb_w", align_bytes=64)
+        nc.vector.tensor_copy(xa_s[:], xs[:].indirect(offs_t[:]))
+        nc.vector.tensor_copy(xa_w[:], xw[:].bitcast(U32).indirect(offs_t[:]))
+
+        w_dealt = [keep.tile([P, S], I32, name="w_dealt%d" % i, align_bytes=64) for i in range(3)]
+        w1s = keep.tile([P, S], U8, name="w1s", align_bytes=64)
+        w23s = keep.tile([P, S], U8, name="w23s", align_bytes=64)
+        deal(w1s, w1s_raw, 0, 4)
+        deal(w_dealt[0], w_raw[0], 2, 4)
+        deal(w_dealt[0], w_raw[0], 0, 2)
+
+        y_bank = [psum.tile([P, S], F32, name="y_bank%d" % t) for t in range(PACK)]
+        h_bank = {(g, c): psum.tile([P, 2, HALF], F32, name="h_bank%d_%d" % (g, c)) for g in range(2) for c in range(2)}
+        for t in SLOT_ORDER:
+            cols = slice(t * P, (t + 1) * P)
+            nc.tensor.matmul_mx(out=y_bank[t][:], lhsT=w_dealt[0][:, cols].bitcast(FP8X4), lhsT_scale=w1s[:, cols],
+                                rhs=xa_w[:].bitcast(FP8X4), rhs_scale=xa_s[:], start=True, stop=True)
+
+        nc.vector.tensor_copy(xb_s[:], xs[:].indirect(two_t[:]))
+        nc.vector.tensor_copy(xb_w[:], xw[:].bitcast(U32).indirect(two_t[:]))
+        deal(w_dealt[2], w_raw[2], 0, 4)
+        deal(w_dealt[1], w_raw[1], 0, 4)
+
+        zb = keep.tile([P, S, PACK], BF16, name="zb", align_bytes=64)
+        deal(w23s, w23s_raw, 0, 4)
+        for t in range(PACK):
+            cols = slice(t * P, (t + 1) * P)
+            for c, (lo, hi) in enumerate(CHUNKS):
+                nc.tensor.matmul_mx(out=h_bank[t // 2, c][:, t % 2, :], lhsT=w_dealt[2][:, cols].bitcast(FP8X4), lhsT_scale=w23s[4:P, cols],
+                                    rhs=xb_w[:, lo:hi].bitcast(FP8X4), rhs_scale=xb_s[:, lo:hi], start=(t % 2 == 0), stop=False)
+
+        pa, pb, ra, rb, dt = {}, {}, {}, {}, {}
+
+        def fetch(t):
+            y = keep.tile([P, S], F32, name="y%d" % t)
+            nc.scalar.copy(y[:], y_bank[t][:])
+            pa[t] = keep.tile([P, W], F32, name="pa%d" % t)
+            pb[t] = keep.tile([P, W], F32, name="pb%d" % t)
+            nc.scalar.activation(pa[t][:], y[:].indirect(n1_t[:]), COPY)
+            nc.scalar.activation(pb[t][:], y[:].indirect(n2_t[:]), COPY)
+
+        def order(t):
+            ra[t] = ring.tile([P, W], F32, name="ra")
+            rb[t] = ring.tile([P, W], F32, name="rb")
+            nc.vector.tensor_tensor(ra[t][:], pa[t][:], pb[t][:], ALU.max)
+            nc.vector.tensor_tensor(rb[t][:], pa[t][:], pb[t][:], ALU.min)
+
+        def put_larger(t):
+            dt[t] = ring.tile([P, S], F32, name="dt", bufs=3)
+            nc.vector.tensor_copy(dt[t][:].indirect(n1_t[:]), ra[t][:])
+
+        def put_smaller(t):
+            nc.vector.tensor_copy(dt[t][:].indirect(n2_t[:]), rb[t][:])
+
+        def scale_round(t, last):
+            if last:
+                nc.vector.tensor_scalar(zb[:, 0:HALF, t], dt[t][:, 0:HALF], gain[:, t : t + 1], None, ALU.mult)
+                nc.scalar.activation(zb[:, HALF:S, t], dt[t][:, HALF:S], COPY, scale=gain[:, t : t + 1])
+            else:
+                nc.scalar.activation(zb[:, :, t], dt[t][:], COPY, scale=gain[:, t : t + 1])
+
+        for t in SLOT_ORDER:
+            fetch(t)
+        for i, t in enumerate(SLOT_ORDER):
+            order(t)
+            if i > 0:
+                put_smaller(SLOT_ORDER[i - 1])
+                scale_round(SLOT_ORDER[i - 1], False)
+            put_larger(t)
+        put_smaller(SLOT_ORDER[-1])
+        scale_round(SLOT_ORDER[-1], True)
+
+        z_w = keep.tile([P, S], U32, name="z_w", align_bytes=64)
+        z_s = keep.tile([P, S], U8, name="z_s", align_bytes=64)
+        for lo in (0, HALF):
+            nc.vector.quantize_mx(out=z_w[:, lo : lo + HALF].bitcast(FP8X4), scales=z_s[:, lo : lo + HALF],
+                                  in_=zb[:, lo : lo + HALF, :].rearrange("p c t -> p (c t)"))
+        for g in range(2):
+            for c, (lo, hi) in enumerate(CHUNKS):
+                for t in (2 * g, 2 * g + 1):
+                    cols = slice(t * P, (t + 1) * P)
+                    nc.tensor.matmul_mx(out=h_bank[g, c][:, t % 2, :], lhsT=w_dealt[1][:, cols].bitcast(FP8X4), lhsT_scale=w23s[:, cols],
+                                        rhs=z_w[:, lo:hi].bitcast(FP8X4), rhs_scale=z_s[:, lo:hi], start=False, stop=(t % 2 == 1))
+
+        h = [keep.tile([P, S], F32, name="h%d" % t) for t in range(PACK)]
+        o_w = keep.tile([P, S], U32, name="o_w", align_bytes=64)
+        o_s = keep.tile([P, S], U8, name="o_s", align_bytes=64)
+        out_rows = out_0.rearrange("(p t) j -> p t j", t=PACK)
+        for c, (lo, hi) in enumerate(CHUNKS):
+            cw = hi - lo
+            o = keep.tile([P, PACK, cw], F32, name="o%d" % c)
+            for g in range(2):
+                pair = slice(2 * g, 2 * g + 2)
+                u = keep.tile([P, 2, cw], F32, name="u%d_%d" % (c, g))
+                v = keep.tile([P, 2, cw], F32, name="v%d_%d" % (c, g))
+                for t in (2 * g, 2 * g + 1):
+                    if c == 0:
+                        for d, (dlo, dhi) in enumerate(CHUNKS):
+                            if t == 1:
+                                nc.vector.tensor_copy(h[t][:, dlo:dhi], h_bank[g, d][:, t % 2, :])
+                            else:
+                                nc.scalar.copy(h[t][:, dlo:dhi], h_bank[g, d][:, t % 2, :])
+                for dst, lst, k in ((u, n3_t, 0), (v, n4_t, 1)):
+                    for t in (2 * g, 2 * g + 1):
+                        looked_up = h[t][:].indirect(lst[:, lo // 16 : hi // 16])
+                        if (c, t, k) in ON_VECTOR:
+                            nc.vector.tensor_copy(dst[:, t % 2, :], looked_up)
+                        else:
+                            nc.scalar.activation(dst[:, t % 2, :], looked_up, COPY)
+                a = keep.tile([P, 2, cw], F32, name="a%d_%d" % (c, g))
+                b = keep.tile([P, 2, cw], F32, name="b%d_%d" % (c, g))
+                s = keep.tile([P, 2, cw], F32, name="s%d_%d" % (c, g))
+                nc.vector.tensor_tensor(a[:], h_bank[g, c][:], u[:], ALU.subtract)
+                nc.vector.tensor_tensor(b[:], v[:], h_bank[g, c][:], ALU.subtract)
+                nc.vector.scalar_tensor_tensor(s[:], b[:], 0.0, a[:], ALU.max, ALU.min)
+                nc.vector.scalar_tensor_tensor(o[:, pair, :], b[:], 0.0, s[:], ALU.min, ALU.max)
+                nc.sync.dma_start(out=out_rows[:, pair, lo:hi], in_=o[:, pair, :])
+            ob = keep.tile([P, cw, PACK], BF16, name="ob%d" % c, align_bytes=64)
+            nc.vector.tensor_copy(ob[:].rearrange("p (c i) t -> p c t i", i=4), o[:].rearrange("p t (c i) -> p c t i", i=4))
+            nc.vector.quantize_mx(out=o_w[:, lo:hi].bitcast(FP8X4), scales=o_s[:, lo:hi], in_=ob[:].rearrange("p c t -> p (c t)"))
+            nc.sync.dma_start(out=words_view(out_1)[:, lo:hi], in_=o_w[:, lo:hi].bitcast(I32))
+        for q in range(4):
+            queue = nc.scalar if q % 2 == 0 else nc.sync
+            queue.dma_start(out=out_2[0][4 * q : 4 * q + 4, :].bitcast(I32), in_=o_s[32 * q : 32 * q + 4, :].bitcast(I32))

@@ -22,7 +22,8 @@ FLOPS = 3 * 2 * 512 * 512 * 512
 SLOT_ORDER = (2, 0, 1, 3)
 CHUNKS = ((0, 256), (256, 512))
 HALF = 256
-ON_VECTOR = ((0, 1, 0), (0, 1, 1))
+ON_VECTOR = ((0, 1, 0), (0, 1, 1), (0, 3, 1), (1, 1, 1))
+PIECES = ((0, 256), (256, 384), (384, 512))
 
 
 def tile_picked_mixinorderminmod_none_po_kernel(tc, x_words, x_scales, w1_words, w1_scales, gn, w2_words, w2_scales, w3_words, w3_scales,
@@ -38,8 +39,11 @@ def tile_picked_mixinorderminmod_none_po_kernel(tc, x_words, x_scales, w1_words,
                             in_=dram[0][4 * q : 4 * q + 4, :].bitcast(I32))
 
     def deal(dst, src, lo, hi):
-        nc.vector.tensor_copy(out=dst[:].rearrange("p (t m) -> p t m", t=PACK)[:, lo:hi, :],
-                              in_=src[:].rearrange("p (m t) -> p t m", t=PACK)[:, lo:hi, :])
+        nc.vector.tensor_copy(out=dst[:].rearrange("p (t m) -> p m t", t=PACK)[:, :, lo:hi],
+                              in_=src[:].rearrange("p (m t) -> p m t", t=PACK)[:, :, lo:hi])
+
+    def deal_bytes(dst, src):
+        nc.vector.tensor_copy(out=dst[:].rearrange("p (t m) -> p t m", t=PACK), in_=src[:].rearrange("p (m t) -> p t m", t=PACK))
 
     with ExitStack() as ctx:
         lists = ctx.enter_context(tc.tile_pool(name="lists", bufs=1))
@@ -77,10 +81,10 @@ def tile_picked_mixinorderminmod_none_po_kernel(tc, x_words, x_scales, w1_words,
         two_t = list_tile(two, "two_t")
         n1_t = list_tile(n1, "n1_t")
         n2_t = list_tile(n2, "n2_t")
-        load_scale_rows(nc.sync, w23s_raw, 0, w2_scales)
-        load_scale_rows(nc.sync, w23s_raw, 4, w3_scales)
         gain = keep.tile([P, PACK], F32, name="gain")
         nc.sync.dma_start(out=gain[:], in_=gn.rearrange("(p t) o -> p (t o)", t=PACK))
+        load_scale_rows(nc.sync, w23s_raw, 0, w2_scales)
+        load_scale_rows(nc.sync, w23s_raw, 4, w3_scales)
         n3_t = list_tile(n3, "n3_t")
         n4_t = list_tile(n4, "n4_t")
 
@@ -93,8 +97,7 @@ def tile_picked_mixinorderminmod_none_po_kernel(tc, x_words, x_scales, w1_words,
 
         w_dealt = [keep.tile([P, S], I32, name="w_dealt%d" % i, align_bytes=64) for i in range(3)]
         w1s = keep.tile([P, S], U8, name="w1s", align_bytes=64)
-        w23s = keep.tile([P, S], U8, name="w23s", align_bytes=64)
-        deal(w1s, w1s_raw, 0, 4)
+        deal_bytes(w1s, w1s_raw)
         deal(w_dealt[0], w_raw[0], 2, 4)
         deal(w_dealt[0], w_raw[0], 0, 2)
 
@@ -111,18 +114,12 @@ def tile_picked_mixinorderminmod_none_po_kernel(tc, x_words, x_scales, w1_words,
         deal(w_dealt[1], w_raw[1], 0, 4)
 
         zb = keep.tile([P, S, PACK], BF16, name="zb", align_bytes=64)
-        deal(w23s, w23s_raw, 0, 4)
-        for t in range(PACK):
-            cols = slice(t * P, (t + 1) * P)
-            for c, (lo, hi) in enumerate(CHUNKS):
-                nc.tensor.matmul_mx(out=h_bank[t // 2, c][:, t % 2, :], lhsT=w_dealt[2][:, cols].bitcast(FP8X4), lhsT_scale=w23s[4:P, cols],
-                                    rhs=xb_w[:, lo:hi].bitcast(FP8X4), rhs_scale=xb_s[:, lo:hi], start=(t % 2 == 0), stop=False)
-
         pa, pb, ra, rb, dt = {}, {}, {}, {}, {}
 
         def fetch(t):
             y = keep.tile([P, S], F32, name="y%d" % t)
-            nc.scalar.copy(y[:], y_bank[t][:])
+            for lo, hi in CHUNKS:
+                nc.scalar.copy(y[:, lo:hi], y_bank[t][:, lo:hi])
             pa[t] = keep.tile([P, W], F32, name="pa%d" % t)
             pb[t] = keep.tile([P, W], F32, name="pb%d" % t)
             nc.scalar.activation(pa[t][:], y[:].indirect(n1_t[:]), COPY)
@@ -130,7 +127,7 @@ def tile_picked_mixinorderminmod_none_po_kernel(tc, x_words, x_scales, w1_words,
 
         def order(t):
             ra[t] = ring.tile([P, W], F32, name="ra")
-            rb[t] = ring.tile([P, W], F32, name="rb")
+            rb[t] = ring.tile([P, W], F32, name="rb", align_bytes=64)
             nc.vector.tensor_tensor(ra[t][:], pa[t][:], pb[t][:], ALU.max)
             nc.vector.tensor_tensor(rb[t][:], pa[t][:], pb[t][:], ALU.min)
 
@@ -156,6 +153,14 @@ def tile_picked_mixinorderminmod_none_po_kernel(tc, x_words, x_scales, w1_words,
                 put_smaller(SLOT_ORDER[i - 1])
                 scale_round(SLOT_ORDER[i - 1], False)
             put_larger(t)
+        w23s = ring.tile([P, S], U8, name="w23s", tag="rb", align_bytes=64)
+        deal_bytes(w23s, w23s_raw)
+        for t in range(PACK):
+            cols = slice(t * P, (t + 1) * P)
+            for c, (lo, hi) in enumerate(CHUNKS):
+                nc.tensor.matmul_mx(out=h_bank[t // 2, c][:, t % 2, :], lhsT=w_dealt[2][:, cols].bitcast(FP8X4), lhsT_scale=w23s[4:P, cols],
+                                    rhs=xb_w[:, lo:hi].bitcast(FP8X4), rhs_scale=xb_s[:, lo:hi], start=(t % 2 == 0), stop=False)
+
         put_smaller(SLOT_ORDER[-1])
         scale_round(SLOT_ORDER[-1], True)
 
@@ -175,15 +180,32 @@ def tile_picked_mixinorderminmod_none_po_kernel(tc, x_words, x_scales, w1_words,
         o_w = keep.tile([P, S], U32, name="o_w", align_bytes=64)
         o_s = keep.tile([P, S], U8, name="o_s", align_bytes=64)
         out_rows = out_0.rearrange("(p t) j -> p t j", t=PACK)
-        for c, (lo, hi) in enumerate(CHUNKS):
+        ob = [keep.tile([P, HALF, PACK], BF16, name="ob%d" % c, align_bytes=64) for c in range(2)]
+
+        def round_planes(engine, o, lo, hi, first, last):
+            dst = ob[lo // HALF][:, lo % HALF : lo % HALF + hi - lo, first:last].rearrange("p (c i) t -> p c t i", i=4)
+            src = o[:, first:last, :].rearrange("p t (c i) -> p c t i", i=4)
+            if engine == "vector":
+                nc.vector.tensor_copy(dst, src)
+            else:
+                nc.scalar.copy(dst, src)
+
+        def quantise_out(c):
+            lo, hi = CHUNKS[c]
+            nc.vector.quantize_mx(out=o_w[:, lo:hi].bitcast(FP8X4), scales=o_s[:, lo:hi], in_=ob[c][:].rearrange("p c t -> p (c t)"))
+            nc.sync.dma_start(out=words_view(out_1)[:, lo:hi], in_=o_w[:, lo:hi].bitcast(I32))
+
+        for e, (lo, hi) in enumerate(PIECES):
             cw = hi - lo
-            o = keep.tile([P, PACK, cw], F32, name="o%d" % c)
+            c = lo // HALF
+            inner = slice(lo % HALF, lo % HALF + cw)
+            o = keep.tile([P, PACK, cw], F32, name="o%d" % e)
             for g in range(2):
                 pair = slice(2 * g, 2 * g + 2)
-                u = keep.tile([P, 2, cw], F32, name="u%d_%d" % (c, g))
-                v = keep.tile([P, 2, cw], F32, name="v%d_%d" % (c, g))
+                u = keep.tile([P, 2, cw], F32, name="u%d_%d" % (e, g))
+                v = keep.tile([P, 2, cw], F32, name="v%d_%d" % (e, g))
                 for t in (2 * g, 2 * g + 1):
-                    if c == 0:
+                    if e == 0:
                         for d, (dlo, dhi) in enumerate(CHUNKS):
                             if t == 1:
                                 nc.vector.tensor_copy(h[t][:, dlo:dhi], h_bank[g, d][:, t % 2, :])
@@ -192,22 +214,26 @@ def tile_picked_mixinorderminmod_none_po_kernel(tc, x_words, x_scales, w1_words,
                 for dst, lst, k in ((u, n3_t, 0), (v, n4_t, 1)):
                     for t in (2 * g, 2 * g + 1):
                         looked_up = h[t][:].indirect(lst[:, lo // 16 : hi // 16])
-                        if (c, t, k) in ON_VECTOR:
+                        if (e, t, k) in ON_VECTOR:
                             nc.vector.tensor_copy(dst[:, t % 2, :], looked_up)
                         else:
                             nc.scalar.activation(dst[:, t % 2, :], looked_up, COPY)
-                a = keep.tile([P, 2, cw], F32, name="a%d_%d" % (c, g))
-                b = keep.tile([P, 2, cw], F32, name="b%d_%d" % (c, g))
-                s = keep.tile([P, 2, cw], F32, name="s%d_%d" % (c, g))
-                nc.vector.tensor_tensor(a[:], h_bank[g, c][:], u[:], ALU.subtract)
-                nc.vector.tensor_tensor(b[:], v[:], h_bank[g, c][:], ALU.subtract)
+                a = keep.tile([P, 2, cw], F32, name="a", bufs=2)
+                b = keep.tile([P, 2, cw], F32, name="b", bufs=2)
+                s = keep.tile([P, 2, cw], F32, name="s", bufs=2)
+                nc.vector.tensor_tensor(a[:], h_bank[g, c][:, :, inner], u[:], ALU.subtract)
+                nc.vector.tensor_tensor(b[:], v[:], h_bank[g, c][:, :, inner], ALU.subtract)
                 nc.vector.scalar_tensor_tensor(s[:], b[:], 0.0, a[:], ALU.max, ALU.min)
                 nc.vector.scalar_tensor_tensor(o[:, pair, :], b[:], 0.0, s[:], ALU.min, ALU.max)
                 nc.sync.dma_start(out=out_rows[:, pair, lo:hi], in_=o[:, pair, :])
-            ob = keep.tile([P, cw, PACK], BF16, name="ob%d" % c, align_bytes=64)
-            nc.vector.tensor_copy(ob[:].rearrange("p (c i) t -> p c t i", i=4), o[:].rearrange("p t (c i) -> p c t i", i=4))
-            nc.vector.quantize_mx(out=o_w[:, lo:hi].bitcast(FP8X4), scales=o_s[:, lo:hi], in_=ob[:].rearrange("p c t -> p (c t)"))
-            nc.sync.dma_start(out=words_view(out_1)[:, lo:hi], in_=o_w[:, lo:hi].bitcast(I32))
+                if e == 2:
+                    round_planes("scalar" if g == 0 else "vector", o, lo, hi, 2 * g, 2 * g + 2)
+            if e == 0:
+                round_planes("vector", o, lo, hi, 0, PACK)
+                quantise_out(0)
+            if e == 1:
+                round_planes("scalar", o, lo, hi, 0, PACK)
+        quantise_out(1)
         for q in range(4):
             queue = nc.scalar if q % 2 == 0 else nc.sync
             queue.dma_start(out=out_2[0][4 * q : 4 * q + 4, :].bitcast(I32), in_=o_s[32 * q : 32 * q + 4, :].bitcast(I32))

@@ -22,7 +22,7 @@ FLOPS = 3 * 2 * 512 * 512 * 512
 SLOT_ORDER = (2, 0, 1, 3)
 CHUNKS = ((0, 256), (256, 512))
 HALF = 256
-ON_VECTOR = ((0, 1, 0), (0, 1, 1), (0, 3, 1), (1, 1, 1))
+ON_VECTOR = ((0, 1, 0), (0, 1, 1), (0, 3, 1))
 PIECES = ((0, 256), (256, 384), (384, 512))
 
 
@@ -177,24 +177,14 @@ def tile_picked_mixinorderminmod_none_po_kernel(tc, x_words, x_scales, w1_words,
                                         rhs=z_w[:, lo:hi].bitcast(FP8X4), rhs_scale=z_s[:, lo:hi], start=False, stop=(t % 2 == 1))
 
         h = [keep.tile([P, S], F32, name="h%d" % t) for t in range(PACK)]
-        o_w = keep.tile([P, S], U32, name="o_w", align_bytes=64)
-        o_s = keep.tile([P, S], U8, name="o_s", align_bytes=64)
         out_rows = out_0.rearrange("(p t) j -> p t j", t=PACK)
         ob = [keep.tile([P, HALF, PACK], BF16, name="ob%d" % c, align_bytes=64) for c in range(2)]
 
-        def round_planes(engine, o, lo, hi, first, last):
-            dst = ob[lo // HALF][:, lo % HALF : lo % HALF + hi - lo, first:last].rearrange("p (c i) t -> p c t i", i=4)
-            src = o[:, first:last, :].rearrange("p t (c i) -> p c t i", i=4)
-            if engine == "vector":
-                nc.vector.tensor_copy(dst, src)
-            else:
-                nc.scalar.copy(dst, src)
+        def round_piece(copy, o, lo, hi):
+            dst = ob[lo // HALF][:, lo % HALF : lo % HALF + hi - lo, :]
+            copy(dst.rearrange("p (c i) t -> p c t i", i=4), o[:].rearrange("p t (c i) -> p c t i", i=4))
 
-        def quantise_out(c):
-            lo, hi = CHUNKS[c]
-            nc.vector.quantize_mx(out=o_w[:, lo:hi].bitcast(FP8X4), scales=o_s[:, lo:hi], in_=ob[c][:].rearrange("p c t -> p (c t)"))
-            nc.sync.dma_start(out=words_view(out_1)[:, lo:hi], in_=o_w[:, lo:hi].bitcast(I32))
-
+        results = []
         for e, (lo, hi) in enumerate(PIECES):
             cw = hi - lo
             c = lo // HALF
@@ -218,7 +208,7 @@ def tile_picked_mixinorderminmod_none_po_kernel(tc, x_words, x_scales, w1_words,
                             nc.vector.tensor_copy(dst[:, t % 2, :], looked_up)
                         else:
                             nc.scalar.activation(dst[:, t % 2, :], looked_up, COPY)
-                a = keep.tile([P, 2, cw], F32, name="a", bufs=2)
+                a = keep.tile([P, 2, cw], F32, name="a", bufs=2, align_bytes=64)
                 b = keep.tile([P, 2, cw], F32, name="b", bufs=2)
                 s = keep.tile([P, 2, cw], F32, name="s", bufs=2)
                 nc.vector.tensor_tensor(a[:], h_bank[g, c][:, :, inner], u[:], ALU.subtract)
@@ -226,14 +216,17 @@ def tile_picked_mixinorderminmod_none_po_kernel(tc, x_words, x_scales, w1_words,
                 nc.vector.scalar_tensor_tensor(s[:], b[:], 0.0, a[:], ALU.max, ALU.min)
                 nc.vector.scalar_tensor_tensor(o[:, pair, :], b[:], 0.0, s[:], ALU.min, ALU.max)
                 nc.sync.dma_start(out=out_rows[:, pair, lo:hi], in_=o[:, pair, :])
-                if e == 2:
-                    round_planes("scalar" if g == 0 else "vector", o, lo, hi, 2 * g, 2 * g + 2)
-            if e == 0:
-                round_planes("vector", o, lo, hi, 0, PACK)
-                quantise_out(0)
-            if e == 1:
-                round_planes("scalar", o, lo, hi, 0, PACK)
-        quantise_out(1)
+            results.append(o)
+        for e, (lo, hi) in enumerate(PIECES):
+            round_piece(nc.vector.tensor_copy if e == len(PIECES) - 1 else nc.scalar.copy, results[e], lo, hi)
+        o_s = keep.tile([P, S], U8, name="o_s", tag="a", bufs=2, align_bytes=64)
+        for c, (lo, hi) in enumerate(CHUNKS):
+            if c == 0:
+                o_w = keep.tile([P, HALF], U32, name="o_w0", tag="a", bufs=2, align_bytes=64)
+            else:
+                o_w = keep.tile([P, HALF], U32, name="o_w1", align_bytes=64)
+            nc.vector.quantize_mx(out=o_w[:].bitcast(FP8X4), scales=o_s[:, lo:hi], in_=ob[c][:].rearrange("p c t -> p (c t)"))
+            nc.sync.dma_start(out=words_view(out_1)[:, lo:hi], in_=o_w[:].bitcast(I32))
         for q in range(4):
             queue = nc.scalar if q % 2 == 0 else nc.sync
             queue.dma_start(out=out_2[0][4 * q : 4 * q + 4, :].bitcast(I32), in_=o_s[32 * q : 32 * q + 4, :].bitcast(I32))

@@ -61,24 +61,18 @@ def tile_picked_mixinorderminmod_none_po_kernel(tc, x_words, x_scales, w1_words,
         w23s_raw = keep.tile([P, S], U8, name="w23s_raw", align_bytes=64)
         nc.vector.memset(xs[:, 0 : T // 2].bitcast(I32), 0)
         nc.gpsimd.memset(xs[:, T // 2 : T].bitcast(I32), 0)
+        nc.gpsimd.memset(w1s_raw[:].bitcast(I32), 0)
         nc.gpsimd.memset(w23s_raw[:].bitcast(I32), 0)
 
-        def load_w1_scales(queue, q):
-            rows = w1_scales[0][4 * q : 4 * q + 4, :].bitcast(I32)
-            queue.dma_start(out=w1s_raw[32 * q : 32 * q + 32, :].bitcast(I32), in_=rows.unsqueeze(0).to_broadcast([8, 4, S // 4]))
-
         offs_t = list_tile(offs, "offs_t")
-        load_w1_scales(nc.scalar, 0)
-        load_w1_scales(nc.scalar, 1)
-        xw = keep.tile([P, T], I32, name="xw", align_bytes=64)
-        nc.scalar.dma_start(out=xw[:], in_=words_view(x_words))
+        two_t = list_tile(two, "two_t")
         load_scale_rows(nc.sync, xs, 0, x_scales)
-        load_w1_scales(nc.sync, 2)
-        load_w1_scales(nc.sync, 3)
+        xw = keep.tile([P, T], I32, name="xw", align_bytes=64)
+        nc.sync.dma_start(out=xw[:], in_=words_view(x_words))
+        load_scale_rows(nc.sync, w1s_raw, 0, w1_scales)
         w_raw = [keep.tile([P, S], I32, name="w_raw%d" % i, align_bytes=64) for i in range(3)]
         for i, words in ((0, w1_words), (2, w3_words), (1, w2_words)):
-            nc.scalar.dma_start(out=w_raw[i][:], in_=words_view(words))
-        two_t = list_tile(two, "two_t")
+            nc.sync.dma_start(out=w_raw[i][:], in_=words_view(words))
         n1_t = list_tile(n1, "n1_t")
         n2_t = list_tile(n2, "n2_t")
         gain = keep.tile([P, PACK], F32, name="gain")
@@ -91,8 +85,8 @@ def tile_picked_mixinorderminmod_none_po_kernel(tc, x_words, x_scales, w1_words,
         xa_s = keep.tile([P, S], U8, name="xa_s", align_bytes=64)
         xb_s = keep.tile([P, S], U8, name="xb_s", align_bytes=64)
         xa_w = keep.tile([P, S], U32, name="xa_w", align_bytes=64)
-        xb_w = keep.tile([P, S], U32, name="xb_w", align_bytes=64)
         nc.vector.tensor_copy(xa_s[:], xs[:].indirect(offs_t[:]))
+        nc.vector.tensor_copy(xb_s[:], xs[:].indirect(two_t[:]))
         nc.vector.tensor_copy(xa_w[:], xw[:].bitcast(U32).indirect(offs_t[:]))
 
         w_dealt = [keep.tile([P, S], I32, name="w_dealt%d" % i, align_bytes=64) for i in range(3)]
@@ -108,7 +102,7 @@ def tile_picked_mixinorderminmod_none_po_kernel(tc, x_words, x_scales, w1_words,
             nc.tensor.matmul_mx(out=y_bank[t][:], lhsT=w_dealt[0][:, cols].bitcast(FP8X4), lhsT_scale=w1s[:, cols],
                                 rhs=xa_w[:].bitcast(FP8X4), rhs_scale=xa_s[:], start=True, stop=True)
 
-        nc.vector.tensor_copy(xb_s[:], xs[:].indirect(two_t[:]))
+        xb_w = keep.tile([P, S], U32, name="xb_w", tag="w_raw0", align_bytes=64)
         nc.vector.tensor_copy(xb_w[:], xw[:].bitcast(U32).indirect(two_t[:]))
         deal(w_dealt[2], w_raw[2], 0, 4)
         deal(w_dealt[1], w_raw[1], 0, 4)
@@ -123,7 +117,10 @@ def tile_picked_mixinorderminmod_none_po_kernel(tc, x_words, x_scales, w1_words,
             pa[t] = keep.tile([P, W], F32, name="pa%d" % t)
             pb[t] = keep.tile([P, W], F32, name="pb%d" % t)
             nc.scalar.activation(pa[t][:], y[:].indirect(n1_t[:]), COPY)
-            nc.scalar.activation(pb[t][:], y[:].indirect(n2_t[:]), COPY)
+            if t == SLOT_ORDER[0]:
+                nc.vector.tensor_copy(pb[t][:], y[:].indirect(n2_t[:]))
+            else:
+                nc.scalar.activation(pb[t][:], y[:].indirect(n2_t[:]), COPY)
 
         def order(t):
             ra[t] = ring.tile([P, W], F32, name="ra")

@@ -22,7 +22,7 @@ FLOPS = 3 * 2 * 512 * 512 * 512
 SLOT_ORDER = (2, 0, 1, 3)
 CHUNKS = ((0, 256), (256, 512))
 HALF = 256
-ON_VECTOR = ((0, 1, 0), (0, 1, 1), (0, 3, 1))
+ON_VECTOR = ((0, 1, 0), (0, 1, 1), (1, 1, 1))
 PIECES = ((0, 256), (256, 384), (384, 512))
 
 
@@ -59,10 +59,8 @@ def tile_picked_mixinorderminmod_none_po_kernel(tc, x_words, x_scales, w1_words,
         xs = keep.tile([P, T], U8, name="xs", align_bytes=64)
         w1s_raw = keep.tile([P, S], U8, name="w1s_raw", align_bytes=64)
         w23s_raw = keep.tile([P, S], U8, name="w23s_raw", align_bytes=64)
-        nc.vector.memset(xs[:, 0 : T // 2].bitcast(I32), 0)
-        nc.gpsimd.memset(xs[:, T // 2 : T].bitcast(I32), 0)
-        nc.gpsimd.memset(w1s_raw[:].bitcast(I32), 0)
-        nc.gpsimd.memset(w23s_raw[:].bitcast(I32), 0)
+        for tile in (xs, w1s_raw, w23s_raw):
+            nc.vector.memset(tile[:].bitcast(I32), 0)
 
         offs_t = list_tile(offs, "offs_t")
         two_t = list_tile(two, "two_t")
@@ -217,13 +215,15 @@ def tile_picked_mixinorderminmod_none_po_kernel(tc, x_words, x_scales, w1_words,
         for e, (lo, hi) in enumerate(PIECES):
             round_piece(nc.vector.tensor_copy if e == len(PIECES) - 1 else nc.scalar.copy, results[e], lo, hi)
         o_s = keep.tile([P, S], U8, name="o_s", tag="a", bufs=2, align_bytes=64)
-        for c, (lo, hi) in enumerate(CHUNKS):
-            if c == 0:
-                o_w = keep.tile([P, HALF], U32, name="o_w0", tag="a", bufs=2, align_bytes=64)
-            else:
-                o_w = keep.tile([P, HALF], U32, name="o_w1", align_bytes=64)
-            nc.vector.quantize_mx(out=o_w[:].bitcast(FP8X4), scales=o_s[:, lo:hi], in_=ob[c][:].rearrange("p c t -> p (c t)"))
-            nc.sync.dma_start(out=words_view(out_1)[:, lo:hi], in_=o_w[:].bitcast(I32))
+        last_lo = PIECES[-1][0]
+        o_w_early = keep.tile([P, last_lo], U32, name="o_w_early", tag="a", bufs=2, align_bytes=64)
+        o_w_last = keep.tile([P, S - last_lo], U32, name="o_w_last", align_bytes=64)
+        for lo, hi in PIECES:
+            codes = o_w_early[:, lo:hi] if lo < last_lo else o_w_last[:]
+            rounded = ob[lo // HALF][:, lo % HALF : lo % HALF + hi - lo, :]
+            nc.vector.quantize_mx(out=codes.bitcast(FP8X4), scales=o_s[:, lo:hi], in_=rounded.rearrange("p c t -> p (c t)"))
+        nc.sync.dma_start(out=words_view(out_1)[:, last_lo:S], in_=o_w_last[:].bitcast(I32))
+        nc.scalar.dma_start(out=words_view(out_1)[:, 0:last_lo], in_=o_w_early[:].bitcast(I32))
         for q in range(4):
             queue = nc.scalar if q % 2 == 0 else nc.sync
             queue.dma_start(out=out_2[0][4 * q : 4 * q + 4, :].bitcast(I32), in_=o_s[32 * q : 32 * q + 4, :].bitcast(I32))

from contextlib import ExitStack

import concourse.mybir as mybir

F32 = mybir.dt.float32
BF16 = mybir.dt.bfloat16
I32 = mybir.dt.int32
U32 = mybir.dt.uint32
U16 = mybir.dt.uint16
U8 = mybir.dt.uint8
FP8X4 = mybir.dt.float8_e4m3fn_x4
ALU = mybir.AluOpType
COPY = mybir.ActivationFunctionType.Copy

P = 128
PACK = 4
T = 2048
S = 512
W = 256
FLOPS = 3 * 2 * 512 * 512 * 512

SLOT_ORDER = (2, 0, 1, 3)
CHUNKS = ((0, 256), (256, 512))
HALF = 256
ON_VECTOR = ((0, 1, 0), (0, 1, 1), (1, 1, 1))
PIECES = ((0, 256), (256, 384), (384, 512))


def tile_picked_mixinorderminmod_none_po_kernel(tc, x_words, x_scales, w1_words, w1_scales, gn, w2_words, w2_scales, w3_words, w3_scales,
                        offs, n1, n2, two, n3, n4, out_0, out_1, out_2):
    nc = tc.nc

    def words_view(dram):
        return dram[0].rearrange("p n t -> p (n t)").bitcast(I32)

    def load_scale_rows(queue, tile, first_row, dram):
        for q in range(4):
            queue.dma_start(out=tile[32 * q + first_row : 32 * q + first_row + 4, :].bitcast(I32),
                            in_=dram[0][4 * q : 4 * q + 4, :].bitcast(I32))

    def deal(dst, src, lo, hi):
        nc.vector.tensor_copy(out=dst[:].rearrange("p (t m) -> p m t", t=PACK)[:, :, lo:hi],
                              in_=src[:].rearrange("p (m t) -> p m t", t=PACK)[:, :, lo:hi])

    def deal_bytes(dst, src):
        nc.vector.tensor_copy(out=dst[:].rearrange("p (t m) -> p t m", t=PACK), in_=src[:].rearrange("p (m t) -> p t m", t=PACK))

    with ExitStack() as ctx:
        lists = ctx.enter_context(tc.tile_pool(name="lists", bufs=1))
        keep = ctx.enter_context(tc.tile_pool(name="keep", bufs=1))
        ring = ctx.enter_context(tc.tile_pool(name="ring", bufs=2))
        psum = ctx.enter_context(tc.psum_pool(name="psum", bufs=1))

        def list_tile(dram, name):
            tile = lists.tile([P, dram.shape[1]], U16, name=name)
            nc.sync.dma_start(tile[:], dram)
            return tile

        xs = keep.tile([P, T], U8, name="xs", align_bytes=64)
        w1s_raw = keep.tile([P, S], U8, name="w1s_raw", align_bytes=64)
        w23s_raw = keep.tile([P, S], U8, name="w23s_raw", align_bytes=64)
        for tile in (xs, w1s_raw, w23s_raw):
            nc.vector.memset(tile[:].bitcast(I32), 0)

        offs_t = list_tile(offs, "offs_t")
        two_t = list_tile(two, "two_t")
        load_scale_rows(nc.sync, xs, 0, x_scales)
        xw = keep.tile([P, T], I32, name="xw", align_bytes=64)
        nc.sync.dma_start(out=xw[:], in_=words_view(x_words))
        load_scale_rows(nc.sync, w1s_raw, 0, w1_scales)
        w_raw = [keep.tile([P, S], I32, name="w_raw%d" % i, align_bytes=64) for i in range(3)]
        for i, words in ((0, w1_words), (2, w3_words), (1, w2_words)):
            nc.sync.dma_start(out=w_raw[i][:], in_=words_view(words))
        n1_t = list_tile(n1, "n1_t")
        n2_t = list_tile(n2, "n2_t")
        gain = keep.tile([P, PACK], F32, name="gain")
        nc.sync.dma_start(out=gain[:], in_=gn.rearrange("(p t) o -> p (t o)", t=PACK))
        load_scale_rows(nc.sync, w23s_raw, 0, w2_scales)
        load_scale_rows(nc.sync, w23s_raw, 4, w3_scales)
        n3_t = list_tile(n3, "n3_t")
        n4_t = list_tile(n4, "n4_t")

        xa_s = keep.tile([P, S], U8, name="xa_s", align_bytes=64)
        xb_s = keep.tile([P, S], U8, name="xb_s", align_bytes=64)
        xa_w = keep.tile([P, S], U32, name="xa_w", align_bytes=64)
        nc.vector.tensor_copy(xa_s[:], xs[:].indirect(offs_t[:]))
        nc.vector.tensor_copy(xb_s[:], xs[:].indirect(two_t[:]))
        nc.vector.tensor_copy(xa_w[:], xw[:].bitcast(U32).indirect(offs_t[:]))

        w_dealt = [keep.tile([P, S], I32, name="w_dealt%d" % i, align_bytes=64) for i in range(3)]
        w1s = keep.tile([P, S], U8, name="w1s", align_bytes=64)
        deal_bytes(w1s, w1s_raw)
        deal(w_dealt[0], w_raw[0], 2, 4)
        deal(w_dealt[0], w_raw[0], 0, 2)

        y_bank = [psum.tile([P, S], F32, name="y_bank%d" % t) for t in range(PACK)]
        h_bank = {(g, c): psum.tile([P, 2, HALF], F32, name="h_bank%d_%d" % (g, c)) for g in range(2) for c in range(2)}
        for t in SLOT_ORDER:
            cols = slice(t * P, (t + 1) * P)
            nc.tensor.matmul_mx(out=y_bank[t][:], lhsT=w_dealt[0][:, cols].bitcast(FP8X4), lhsT_scale=w1s[:, cols],
                                rhs=xa_w[:].bitcast(FP8X4), rhs_scale=xa_s[:], start=True, stop=True)

        xb_w = keep.tile([P, S], U32, name="xb_w", tag="w_raw0", align_bytes=64)
        nc.vector.tensor_copy(xb_w[:], xw[:].bitcast(U32).indirect(two_t[:]))
        deal(w_dealt[2], w_raw[2], 0, 4)
        deal(w_dealt[1], w_raw[1], 0, 4)

        zb = keep.tile([P, S, PACK], BF16, name="zb", align_bytes=64)
        pa, pb, ra, rb, dt = {}, {}, {}, {}, {}

        def fetch(t):
            y = keep.tile([P, S], F32, name="y%d" % t)
            for lo, hi in CHUNKS:
                nc.scalar.copy(y[:, lo:hi], y_bank[t][:, lo:hi])
            pa[t] = keep.tile([P, W], F32, name="pa%d" % t)
            pb[t] = keep.tile([P, W], F32, name="pb%d" % t)
            nc.scalar.activation(pa[t][:], y[:].indirect(n1_t[:]), COPY)
            if t == SLOT_ORDER[0]:
                nc.vector.tensor_copy(pb[t][:], y[:].indirect(n2_t[:]))
            else:
                nc.scalar.activation(pb[t][:], y[:].indirect(n2_t[:]), COPY)

        def order(t):
            ra[t] = ring.tile([P, W], F32, name="ra")
            rb[t] = ring.tile([P, W], F32, name="rb", align_bytes=64)
            nc.vector.tensor_tensor(ra[t][:], pa[t][:], pb[t][:], ALU.max)
            nc.vector.tensor_tensor(rb[t][:], pa[t][:], pb[t][:], ALU.min)

        def put_larger(t):
            dt[t] = ring.tile([P, S], F32, name="dt", bufs=3)
            nc.vector.tensor_copy(dt[t][:].indirect(n1_t[:]), ra[t][:])

        def put_smaller(t):
            nc.vector.tensor_copy(dt[t][:].indirect(n2_t[:]), rb[t][:])

        def scale_round(t, last):
            if last:
                nc.vector.tensor_scalar(zb[:, 0:HALF, t], dt[t][:, 0:HALF], gain[:, t : t + 1], None, ALU.mult)
                nc.scalar.activation(zb[:, HALF:S, t], dt[t][:, HALF:S], COPY, scale=gain[:, t : t + 1])
            else:
                nc.scalar.activation(zb[:, :, t], dt[t][:], COPY, scale=gain[:, t : t + 1])

        for t in SLOT_ORDER:
            fetch(t)
        for i, t in enumerate(SLOT_ORDER):
            order(t)
            if i > 0:
                put_smaller(SLOT_ORDER[i - 1])
                scale_round(SLOT_ORDER[i - 1], False)
            put_larger(t)
        w23s = ring.tile([P, S], U8, name="w23s", tag="rb", align_bytes=64)
        deal_bytes(w23s, w23s_raw)
        for t in range(PACK):
            cols = slice(t * P, (t + 1) * P)
            for c, (lo, hi) in enumerate(CHUNKS):
                nc.tensor.matmul_mx(out=h_bank[t // 2, c][:, t % 2, :], lhsT=w_dealt[2][:, cols].bitcast(FP8X4), lhsT_scale=w23s[4:P, cols],
                                    rhs=xb_w[:, lo:hi].bitcast(FP8X4), rhs_scale=xb_s[:, lo:hi], start=(t % 2 == 0), stop=False)

        put_smaller(SLOT_ORDER[-1])
        scale_round(SLOT_ORDER[-1], True)

        z_w = keep.tile([P, S], U32, name="z_w", align_bytes=64)
        z_s = keep.tile([P, S], U8, name="z_s", align_bytes=64)
        for lo in (0, HALF):
            nc.vector.quantize_mx(out=z_w[:, lo : lo + HALF].bitcast(FP8X4), scales=z_s[:, lo : lo + HALF],
                                  in_=zb[:, lo : lo + HALF, :].rearrange("p c t -> p (c t)"))
        for g in range(2):
            for c, (lo, hi) in enumerate(CHUNKS):
                for t in (2 * g, 2 * g + 1):
                    cols = slice(t * P, (t + 1) * P)
                    nc.tensor.matmul_mx(out=h_bank[g, c][:, t % 2, :], lhsT=w_dealt[1][:, cols].bitcast(FP8X4), lhsT_scale=w23s[:, cols],
                                        rhs=z_w[:, lo:hi].bitcast(FP8X4), rhs_scale=z_s[:, lo:hi], start=False, stop=(t % 2 == 1))

        h = [keep.tile([P, S], F32, name="h%d" % t) for t in range(PACK)]
        out_rows = out_0.rearrange("(p t) j -> p t j", t=PACK)
        ob = [keep.tile([P, HALF, PACK], BF16, name="ob%d" % c, align_bytes=64) for c in range(2)]

        def round_piece(copy, o, lo, hi):
            dst = ob[lo // HALF][:, lo % HALF : lo % HALF + hi - lo, :]
            copy(dst.rearrange("p (c i) t -> p c t i", i=4), o[:].rearrange("p t (c i) -> p c t i", i=4))

        results = []
        for e, (lo, hi) in enumerate(PIECES):
            cw = hi - lo
            c = lo // HALF
            inner = slice(lo % HALF, lo % HALF + cw)
            o = keep.tile([P, PACK, cw], F32, name="o%d" % e)
            for g in range(2):
                pair = slice(2 * g, 2 * g + 2)
                u = keep.tile([P, 2, cw], F32, name="u%d_%d" % (e, g))
                v = keep.tile([P, 2, cw], F32, name="v%d_%d" % (e, g))
                for t in (2 * g, 2 * g + 1):
                    if e == 0:
                        for d, (dlo, dhi) in enumerate(CHUNKS):
                            if t == 1:
                                nc.vector.tensor_copy(h[t][:, dlo:dhi], h_bank[g, d][:, t % 2, :])
                            else:
                                nc.scalar.copy(h[t][:, dlo:dhi], h_bank[g, d][:, t % 2, :])
                for dst, lst, k in ((u, n3_t, 0), (v, n4_t, 1)):
                    for t in (2 * g, 2 * g + 1):
                        looked_up = h[t][:].indirect(lst[:, lo // 16 : hi // 16])
                        if (e, t, k) in ON_VECTOR:
                            nc.vector.tensor_copy(dst[:, t % 2, :], looked_up)
                        else:
                            nc.scalar.activation(dst[:, t % 2, :], looked_up, COPY)
                a = keep.tile([P, 2, cw], F32, name="a", bufs=2, align_bytes=64)
                b = keep.tile([P, 2, cw], F32, name="b", bufs=2)
                s = keep.tile([P, 2, cw], F32, name="s", bufs=2)
                nc.vector.tensor_tensor(a[:], h_bank[g, c][:, :, inner], u[:], ALU.subtract)
                nc.vector.tensor_tensor(b[:], v[:], h_bank[g, c][:, :, inner], ALU.subtract)
                nc.vector.scalar_tensor_tensor(s[:], b[:], 0.0, a[:], ALU.max, ALU.min)
                nc.vector.scalar_tensor_tensor(o[:, pair, :], b[:], 0.0, s[:], ALU.min, ALU.max)
                nc.sync.dma_start(out=out_rows[:, pair, lo:hi], in_=o[:, pair, :])
            results.append(o)
        for e, (lo, hi) in enumerate(PIECES):
            round_piece(nc.vector.tensor_copy if e == len(PIECES) - 1 else nc.scalar.copy, results[e], lo, hi)
        o_s = keep.tile([P, S], U8, name="o_s", tag="a", bufs=2, align_bytes=64)
        last_lo = PIECES[-1][0]
        o_w_early = keep.tile([P, last_lo], U32, name="o_w_early", tag="a", bufs=2, align_bytes=64)
        o_w_last = keep.tile([P, S - last_lo], U32, name="o_w_last", align_bytes=64)
        for lo, hi in PIECES:
            codes = o_w_early[:, lo:hi] if lo < last_lo else o_w_last[:]
            rounded = ob[lo // HALF][:, lo % HALF : lo % HALF + hi - lo, :]
            nc.vector.quantize_mx(out=codes.bitcast(FP8X4), scales=o_s[:, lo:hi], in_=rounded.rearrange("p c t -> p (c t)"))
        nc.sync.dma_start(out=words_view(out_1)[:, last_lo:S], in_=o_w_last[:].bitcast(I32))
        nc.scalar.dma_start(out=words_view(out_1)[:, 0:last_lo], in_=o_w_early[:].bitcast(I32))
        for q in range(4):
            queue = nc.scalar if q % 2 == 0 else nc.sync
            queue.dma_start(out=out_2[0][4 * q : 4 * q + 4, :].bitcast(I32), in_=o_s[32 * q : 32 * q + 4, :].bitcast(I32))
